import numpy as np
import ml_dtypes


def mxq(x, axis, fmt="e4m3"):
    dtype, down = {"e4m3": (ml_dtypes.float8_e4m3fn, 7), "e5m2": (ml_dtypes.float8_e5m2, 14)}[fmt]
    v = np.moveaxis(np.asarray(x, np.float32).astype(ml_dtypes.bfloat16).astype(np.float64), axis, -1)
    blocks = v.reshape(v.shape[:-1] + (-1, 32))
    amax = np.abs(blocks).max(-1, keepdims=True)
    byte = np.maximum(np.where(amax > 0, np.frexp(amax)[1] - 1 + 127, 0) - down, 1)
    scale = np.exp2(byte - 127.0)
    codes = (blocks / scale).astype(np.float32).astype(dtype).astype(np.float64)
    return np.moveaxis((codes * scale).reshape(v.shape), -1, axis)


WIDE = False


def mx_kscale(k):
    if not WIDE:
        return np.ones(k)
    levels = np.array([10, -10, 5, -5, 0])
    if k % 512:
        return np.exp2(np.random.permutation(np.resize(levels, k // 32))).repeat(32)
    a = np.empty((k // 512, 16))
    for p in range(k // 512):
        a[p, :8] = np.random.permutation(np.resize(levels, 8))
        for g in range(8):
            far = levels[np.abs(levels - a[p, g]) >= 10]
            a[p, g + 8] = far[np.random.randint(len(far))]
    return np.exp2(a.ravel()).repeat(32)


def f64(x):
    return np.asarray(x).astype(np.float64)


def striped(idx):
    return np.tile(np.asarray(idx).reshape(-1, 16).T, (8, 1)).astype(np.uint16)


def unstriped(offs):
    return offs[:16].T.reshape(-1).astype(np.int64)


E2M1 = np.array([0.0, 0.5, 1.0, 1.5, 2.0, 3.0, 4.0, 6.0, -0.0, -0.5, -1.0, -1.5, -2.0, -3.0, -4.0, -6.0])


def pack_weight(w, fmt):
    k, n = w.shape
    w = f64(np.asarray(w, np.float32).astype(ml_dtypes.bfloat16)).reshape(k // 32, 32, n)
    amax = np.abs(w).max(1)
    if fmt == "e4m3":
        byte = np.frexp(amax)[1] - 1 + 127 - 7
    else:
        mant, ex = np.frexp(amax / 6.0)
        byte = np.where(mant > 0.5, ex, ex - 1) + 127
    byte = np.clip(np.where(amax > 0, byte, 1), 1, 254)
    scaled = (w * np.exp2(127.0 - byte)[:, None, :]).reshape(k, n).astype(np.float32)
    by_word = np.ascontiguousarray(scaled.reshape(k // 512, 128, 4, n).transpose(0, 1, 3, 2))
    if fmt == "e4m3":
        words = by_word.astype(ml_dtypes.float8_e4m3fn).view(np.uint8)
    else:
        c = by_word.astype(ml_dtypes.float4_e2m1fn).view(np.uint8) & 0xF
        words = (c[..., 0::2] | (c[..., 1::2] << 4)).reshape(k // 512, 128, 2 * n)
    return np.ascontiguousarray(words), np.ascontiguousarray(byte.astype(np.uint8).reshape(k // 512, 16, n))


def unpack_weight(words, scales, fmt):
    g, _, n = scales.shape
    words = np.ascontiguousarray(words).reshape(g, 128, n, -1)
    if fmt == "e4m3":
        vals = words.view(ml_dtypes.float8_e4m3fn).astype(np.float64)
    else:
        nib = np.empty((g, 128, n, 4), np.uint8)
        nib[..., 0::2] = words & 0xF
        nib[..., 1::2] = words >> 4
        vals = E2M1[nib]
    vals = vals * np.repeat(np.exp2(scales.astype(np.float64) - 127.0), 8, axis=1)[..., None]
    return vals.transpose(0, 1, 3, 2).reshape(g * 512, n)


def bf(x):
    return np.asarray(x, np.float32).astype(ml_dtypes.bfloat16)


def planes(Y):
    r, m = Y.shape
    b = f64(bf(Y)).reshape(r // 32, 32, m)
    amax = np.abs(b).max(1)
    byte = np.clip(np.where(amax > 0, np.frexp(amax)[1] - 1 + 127 - 7, 1), 1, 254)
    codes = (b * np.exp2(127.0 - byte)[:, None, :]).reshape(r, m).astype(np.float32).astype(ml_dtypes.float8_e4m3fn).view(np.uint8)
    words = codes.reshape(r // 512, 128, 4, m).transpose(0, 1, 3, 2)
    return np.ascontiguousarray(words), np.ascontiguousarray(byte.astype(np.uint8).reshape(r // 512, 16, m))


K, T, J, I, N = 512, 2048, 1024, 512, 512


def setup_inputs():
    n = np.random.standard_normal
    idx = np.random.permutation(T)[:J]
    fk = mx_kscale(K)
    wap = pack_weight(n((K, N)) * 1 / np.sqrt(K) * fk[:, None], "e4m3")
    wbp = pack_weight(n((K, N)) * 1 / np.sqrt(K) * fk[:, None], "e2m1")
    return {
        "xf": (n((K, T)) / fk[:, None]).astype(np.float32),
        "wa_words": wap[0],
        "wa_scales": wap[1],
        "wb_words": wbp[0],
        "wb_scales": wbp[1],
        "rw": (np.random.uniform(0.5, 2.0, (1, J))).astype(np.float32),
        "offs": striped(idx),
    }


def reference(xf, wa_words, wa_scales, wb_words, wb_scales, rw, offs):
    idx = unstriped(offs)
    wau = unpack_weight(wa_words, wa_scales, "e4m3")
    wbu = unpack_weight(wb_words, wb_scales, "e2m1")
    xg = f64(xf)[:, idx]
    xa = xg[:, 0:0 + I]
    xb = xg[:, 512:512 + I]
    xaq = mxq(xa, 0, "e4m3")
    za = wau.T @ xaq
    xbq = mxq(xb, 0, "e4m3")
    zb = wbu.T @ xbq
    z = np.concatenate([za, zb], axis=1)
    y = np.maximum(z, 0.0) * f64(rw)
    words, scales = planes(y)
    return y, words, scales

@@ -1,0 +1,152 @@
+from contextlib import ExitStack
+
+import concourse.mybir as mybir
+from concourse.masks import make_identity
+
+K, T, J, N = 512, 2048, 1024, 512
+FLOPS = 2 * K * N * J
+
+F32 = mybir.dt.float32
+BF16 = mybir.dt.bfloat16
+I32 = mybir.dt.int32
+U32 = mybir.dt.uint32
+U16 = mybir.dt.uint16
+U8 = mybir.dt.uint8
+FP8X4 = mybir.dt.float8_e4m3fn_x4
+FP4X4 = mybir.dt.float4_e2m1fn_x4
+ALU = mybir.AluOpType
+
+P = 128
+PACK = 4
+HALF = J // 2
+CHUNK = 256
+PER_COL = 16
+WA_ROW = 4
+
+
+def tile_list_halves_of_the_list_pl_kernel(tc, xf, wa_words, wa_scales, wb_words, wb_scales, rw, offs, out_0, out_1, out_2):
+    nc = tc.nc
+    halves = [HALF, 0]
+    chunks = [h + c for h in halves for c in range(0, HALF, CHUNK)]
+
+    with ExitStack() as ctx:
+        keep = ctx.enter_context(tc.tile_pool(name="keep", bufs=1))
+        psum = ctx.enter_context(tc.psum_pool(name="psum", bufs=8))
+
+        offsets = keep.tile([P, J // PER_COL], U16, name="offsets")
+        sc_raw = keep.tile([P, N], U8, name="sc_raw", align_bytes=64)
+        nc.vector.memset(sc_raw[:].bitcast(I32), 0)
+
+        nc.sync.dma_start(offsets[:], offs)
+        wb_raw = keep.tile([P, 2 * N], U8, name="wb_raw", align_bytes=64)
+        nc.scalar.dma_start(wb_raw[:].bitcast(I32), wb_words[0].bitcast(I32))
+        for q in range(4):
+            nc.scalar.dma_start(sc_raw[32 * q : 32 * q + 4, :].bitcast(I32), wb_scales[0, 4 * q : 4 * q + 4, :].bitcast(I32))
+        for q in range(4):
+            nc.gpsimd.dma_start(
+                sc_raw[32 * q + WA_ROW : 32 * q + WA_ROW + 4, :].bitcast(I32), wa_scales[0, 4 * q : 4 * q + 4, :].bitcast(I32)
+            )
+        x_rows = xf.rearrange("(p t) n -> t p n", t=PACK)
+        planes = [keep.tile([P, T], F32, name=f"plane{t}") for t in range(PACK)]
+        for t in range(PACK):
+            nc.sync.dma_start(planes[t][:], x_rows[t])
+        wa_raw = keep.tile([P, N], U32, name="wa_raw", align_bytes=64)
+        nc.sync.dma_start(wa_raw[:].bitcast(I32), wa_words[0].rearrange("p n b -> p (n b)").bitcast(I32))
+        rw_cols = keep.tile([P, J // P], F32, name="rw_cols")
+        nc.scalar.dma_start(rw_cols[:], rw.rearrange("o (p m) -> (o p) m", p=P))
+
+        wb_dealt = keep.tile([P, 2 * N], U8, name="wb_dealt", align_bytes=64)
+        nc.vector.tensor_copy(
+            wb_dealt[:].rearrange("p (t q b) -> p t q b", t=PACK, b=2), wb_raw[:].rearrange("p (q t b) -> p t q b", t=PACK, b=2)
+        )
+        sc_dealt = keep.tile([P, N], U8, name="sc_dealt", align_bytes=64)
+        nc.vector.tensor_copy(sc_dealt[:].rearrange("p (t q) -> p t q", t=PACK), sc_raw[:].rearrange("p (q t) -> p t q", t=PACK))
+
+        ident = keep.tile([P, P], F32, name="ident")
+        make_identity(nc, ident[:])
+        rw_all = keep.tile([P, J], F32, name="rw_all")
+        for h in range(2):
+            bank = psum.tile([P, 4, P], F32, name="rw_bank", tag="bank")
+            for m in range(4):
+                nc.tensor.transpose(bank[:, m, :], rw_cols[:, 4 * h + m : 4 * h + m + 1].to_broadcast([P, P]), ident[:])
+            nc.scalar.copy(rw_all[:].rearrange("q (p m) -> q p m", m=8)[:, :, 4 * h : 4 * h + 4], bank[:].rearrange("q m p -> q p m"))
+
+        def gather(out, t, j0, n):
+            nc.vector.tensor_copy(out, planes[t][:].indirect(offsets[:, j0 // PER_COL : (j0 + n) // PER_COL]))
+
+        x_woven = {j0: keep.tile([P, CHUNK, PACK], BF16, name=f"x_woven{j0}", align_bytes=64) for j0 in chunks}
+        low = {h: keep.tile([P, 2, HALF], F32, name=f"low{h}") for h in halves}
+        high = {j0: keep.tile([P, 2, CHUNK], F32, name=f"high{j0}") for j0 in chunks}
+
+        for h in halves:
+            gather(low[h][:, 0, :], 0, h, HALF)
+        for h in halves:
+            gather(low[h][:, 1, :], 1, h, HALF)
+            for c in range(0, HALF, CHUNK):
+                nc.scalar.copy(x_woven[h + c][:, :, 0:2], low[h][:, :, c : c + CHUNK].rearrange("p t n -> p n t"))
+        for j0 in chunks:
+            gather(high[j0][:, 0, :], 2, j0, CHUNK)
+        for j0 in chunks:
+            gather(high[j0][:, 1, :], 3, j0, CHUNK)
+            nc.scalar.copy(x_woven[j0][:, :, 2:4], high[j0][:].rearrange("p t n -> p n t"))
+
+        wa_dealt = keep.tile([P, N], U32, name="wa_dealt", align_bytes=64)
+        nc.vector.tensor_copy(
+            wa_dealt[:].bitcast(I32).rearrange("p (t q) -> p t q", t=PACK), wa_raw[:].bitcast(I32).rearrange("p (q t) -> p t q", t=PACK)
+        )
+
+        x_codes, x_scales = {}, {}
+        for j0 in chunks:
+            codes = keep.tile([P, CHUNK], U32, name=f"x_codes{j0}", align_bytes=64)
+            scales = keep.tile([P, CHUNK], U8, name=f"x_scales{j0}", align_bytes=64)
+            nc.vector.quantize_mx(out=codes[:].bitcast(FP8X4), scales=scales[:], in_=x_woven[j0][:].rearrange("p n t -> p (n t)"))
+            x_codes[j0] = codes
+            x_scales[j0] = scales
+
+        y_rows = out_0.rearrange("(p t) j -> p t j", t=PACK)
+        y_words = out_1[0].rearrange("p j b -> p (j b)").bitcast(I32)
+        y_scales = keep.tile([P, J], U8, name="y_scales", align_bytes=64)
+        y_woven = {}
+        for j0 in chunks:
+            y = keep.tile([P, PACK, CHUNK], F32, name=f"y{j0}")
+            for u in range(2):
+                bank = psum.tile([P, 2, CHUNK], F32, name="z_bank", tag="bank")
+                for s in range(2):
+                    t = 2 * u + s
+                    if j0 >= HALF:
+                        w_codes = wb_dealt[:, 2 * P * t : 2 * P * (t + 1)].bitcast(FP4X4)
+                        w_scales = sc_dealt[:, P * t : P * (t + 1)]
+                    else:
+                        w_codes = wa_dealt[:, P * t : P * (t + 1)].bitcast(FP8X4)
+                        w_scales = sc_dealt[WA_ROW:P, P * t : P * (t + 1)]
+                    nc.tensor.matmul_mx(
+                        out=bank[:, s, :],
+                        lhsT=w_codes,
+                        lhsT_scale=w_scales,
+                        rhs=x_codes[j0][:].bitcast(FP8X4),
+                        rhs_scale=x_scales[j0][:],
+                        start=True,
+                        stop=True,
+                    )
+                nc.vector.scalar_tensor_tensor(
+                    y[:, 2 * u : 2 * u + 2, :],
+                    bank[:],
+                    0.0,
+                    rw_all[:, j0 : j0 + CHUNK].unsqueeze(1).to_broadcast([P, 2, CHUNK]),
+                    ALU.max,
+                    ALU.mult,
+                )
+            nc.sync.dma_start(y_rows[:, :, j0 : j0 + CHUNK], y[:])
+            woven = keep.tile([P, CHUNK, PACK], BF16, name=f"y_woven{j0}", align_bytes=64)
+            nc.scalar.copy(woven[:].rearrange("p (c i) t -> p c t i", i=4), y[:].rearrange("p t (c i) -> p c t i", i=4))
+            y_woven[j0] = woven
+
+        for j0 in chunks:
+            codes = keep.tile([P, CHUNK], U32, name=f"y_codes{j0}", align_bytes=64)
+            nc.vector.quantize_mx(
+                out=codes[:].bitcast(FP8X4), scales=y_scales[:, j0 : j0 + CHUNK], in_=y_woven[j0][:].rearrange("p n t -> p (n t)")
+            )
+            nc.sync.dma_start(y_words[:, j0 : j0 + CHUNK], codes[:].bitcast(I32))
+        for q in range(4):
+            queue = nc.scalar if q % 2 == 0 else nc.sync
+            queue.dma_start(out_2[0, 4 * q : 4 * q + 4, :].bitcast(I32), y_scales[32 * q : 32 * q + 4, :].bitcast(I32))

@@ -21,13 +21,12 @@ PACK = 4
 HALF = J // 2
 CHUNK = 256
 PER_COL = 16
-WA_ROW = 4
 
 
 def tile_list_halves_of_the_list_pl_kernel(tc, xf, wa_words, wa_scales, wb_words, wb_scales, rw, offs, out_0, out_1, out_2):
     nc = tc.nc
-    halves = [HALF, 0]
-    chunks = [h + c for h in halves for c in range(0, HALF, CHUNK)]
+    chunks = list(range(J - CHUNK, -1, -CHUNK))
+    c0, c1, c2, c3 = chunks
 
     with ExitStack() as ctx:
         keep = ctx.enter_context(tc.tile_pool(name="keep", bufs=1))
@@ -35,118 +34,170 @@ def tile_list_halves_of_the_list_pl_kernel(tc, xf, wa_words, wa_scales, wb_words
 
         offsets = keep.tile([P, J // PER_COL], U16, name="offsets")
         sc_raw = keep.tile([P, N], U8, name="sc_raw", align_bytes=64)
-        nc.vector.memset(sc_raw[:].bitcast(I32), 0)
+        nc.gpsimd.memset(sc_raw[32:64, :].bitcast(I32), 0)
+        nc.gpsimd.memset(sc_raw[64:P, :].bitcast(I32), 0)
+        wa_plane = keep.tile([P, N], U8, name="wa_plane", align_bytes=64)
+        nc.gpsimd.memset(wa_plane[:].bitcast(I32), 0)
 
-        nc.sync.dma_start(offsets[:], offs)
-        wb_raw = keep.tile([P, 2 * N], U8, name="wb_raw", align_bytes=64)
-        nc.scalar.dma_start(wb_raw[:].bitcast(I32), wb_words[0].bitcast(I32))
-        for q in range(4):
-            nc.scalar.dma_start(sc_raw[32 * q : 32 * q + 4, :].bitcast(I32), wb_scales[0, 4 * q : 4 * q + 4, :].bitcast(I32))
-        for q in range(4):
-            nc.gpsimd.dma_start(
-                sc_raw[32 * q + WA_ROW : 32 * q + WA_ROW + 4, :].bitcast(I32), wa_scales[0, 4 * q : 4 * q + 4, :].bitcast(I32)
-            )
+        nc.sync.dma_start(sc_raw[0:16, :].bitcast(I32), wb_scales[0].bitcast(I32))
+        nc.sync.dma_start(sc_raw[16:32, :].bitcast(I32), wa_scales[0].bitcast(I32))
+        wb_raw = keep.tile([P, 2 * N], U8, name="wb_raw", tag="w_raw", align_bytes=64)
+        nc.sync.dma_start(wb_raw[:].bitcast(I32), wb_words[0].bitcast(I32))
         x_rows = xf.rearrange("(p t) n -> t p n", t=PACK)
         planes = [keep.tile([P, T], F32, name=f"plane{t}") for t in range(PACK)]
-        for t in range(PACK):
-            nc.sync.dma_start(planes[t][:], x_rows[t])
-        wa_raw = keep.tile([P, N], U32, name="wa_raw", align_bytes=64)
-        nc.sync.dma_start(wa_raw[:].bitcast(I32), wa_words[0].rearrange("p n b -> p (n b)").bitcast(I32))
+        nc.sync.dma_start(planes[0][:], x_rows[0])
+        nc.sync.dma_start(offsets[:], offs)
         rw_cols = keep.tile([P, J // P], F32, name="rw_cols")
-        nc.scalar.dma_start(rw_cols[:], rw.rearrange("o (p m) -> (o p) m", p=P))
+        nc.sync.dma_start(rw_cols[:], rw.rearrange("o (p m) -> (o p) m", p=P))
+        for t in range(1, PACK):
+            nc.sync.dma_start(planes[t][:], x_rows[t])
 
+        wb_plane = keep.tile([P, N], U8, name="wb_plane", align_bytes=64)
+        nc.vector.tensor_copy(wb_plane[:].rearrange("p (t q) -> p t q", t=PACK), sc_raw[:].rearrange("p (q t) -> p t q", t=PACK))
+        for q in range(1, 4):
+            nc.sync.dma_start(wb_plane[32 * q : 32 * q + 4, :].bitcast(I32), wb_plane[4 * q : 4 * q + 4, :].bitcast(I32))
+        for q in range(4):
+            nc.sync.dma_start(wa_plane[32 * q : 32 * q + 4, :].bitcast(I32), wb_plane[16 + 4 * q : 20 + 4 * q, :].bitcast(I32))
         wb_dealt = keep.tile([P, 2 * N], U8, name="wb_dealt", align_bytes=64)
         nc.vector.tensor_copy(
             wb_dealt[:].rearrange("p (t q b) -> p t q b", t=PACK, b=2), wb_raw[:].rearrange("p (q t b) -> p t q b", t=PACK, b=2)
         )
-        sc_dealt = keep.tile([P, N], U8, name="sc_dealt", align_bytes=64)
-        nc.vector.tensor_copy(sc_dealt[:].rearrange("p (t q) -> p t q", t=PACK), sc_raw[:].rearrange("p (q t) -> p t q", t=PACK))
+        wa_raw = keep.tile([P, N], U32, name="wa_raw", tag="w_raw", align_bytes=64)
+        nc.sync.dma_start(wa_raw[:].bitcast(I32), wa_words[0].rearrange("p n b -> p (n b)").bitcast(I32))
+
+        high = {j0: keep.tile([P, 2, CHUNK], F32, name=f"high{j0}", align_bytes=64) for j0 in chunks}
+        low = {h: keep.tile([P, 2, HALF], F32, name=f"low{h}") for h in (HALF, 0)}
 
         ident = keep.tile([P, P], F32, name="ident")
         make_identity(nc, ident[:])
-        rw_all = keep.tile([P, J], F32, name="rw_all")
+        rw_rest = keep.tile([P, c0], F32, name="rw_rest")
+        rw_first = high[c3][:, 1, :]
+        split = c0 // 8
         for h in range(2):
             bank = psum.tile([P, 4, P], F32, name="rw_bank", tag="bank")
             for m in range(4):
                 nc.tensor.transpose(bank[:, m, :], rw_cols[:, 4 * h + m : 4 * h + m + 1].to_broadcast([P, P]), ident[:])
-            nc.scalar.copy(rw_all[:].rearrange("q (p m) -> q p m", m=8)[:, :, 4 * h : 4 * h + 4], bank[:].rearrange("q m p -> q p m"))
+            by_slot = bank[:].rearrange("q m p -> q p m")
+            nc.scalar.copy(rw_first.rearrange("q (p m) -> q p m", m=8)[:, :, 4 * h : 4 * h + 4], by_slot[:, split:P, :])
+            nc.scalar.copy(rw_rest[:].rearrange("q (p m) -> q p m", m=8)[:, :, 4 * h : 4 * h + 4], by_slot[:, 0:split, :])
+
+        def rw_slots(j):
+            return rw_first[:, j - c0 : j - c0 + P] if j >= c0 else rw_rest[:, j : j + P]
 
         def gather(out, t, j0, n):
             nc.vector.tensor_copy(out, planes[t][:].indirect(offsets[:, j0 // PER_COL : (j0 + n) // PER_COL]))
 
-        x_woven = {j0: keep.tile([P, CHUNK, PACK], BF16, name=f"x_woven{j0}", align_bytes=64) for j0 in chunks}
-        low = {h: keep.tile([P, 2, HALF], F32, name=f"low{h}") for h in halves}
-        high = {j0: keep.tile([P, 2, CHUNK], F32, name=f"high{j0}") for j0 in chunks}
+        pieces = [(c0, P), (c0 + P, P), (c1, CHUNK), (c2, CHUNK), (c3, CHUNK)]
+        x_woven = {j: keep.tile([P, n, PACK], BF16, name=f"x_woven{j}", align_bytes=64)[:] for j, n in pieces[1:]}
+        x_woven[c0] = high[c2][:, 1, :].bitcast(BF16).rearrange("p (n t) -> p n t", t=PACK)
 
-        for h in halves:
+        for h in low:
             gather(low[h][:, 0, :], 0, h, HALF)
-        for h in halves:
+        for h in low:
             gather(low[h][:, 1, :], 1, h, HALF)
-            for c in range(0, HALF, CHUNK):
-                nc.scalar.copy(x_woven[h + c][:, :, 0:2], low[h][:, :, c : c + CHUNK].rearrange("p t n -> p n t"))
+            for j, n in pieces:
+                if h <= j < h + HALF:
+                    nc.scalar.copy(x_woven[j][:, :, 0:2], low[h][:, :, j - h : j - h + n].rearrange("p t n -> p n t"))
         for j0 in chunks:
             gather(high[j0][:, 0, :], 2, j0, CHUNK)
-        for j0 in chunks:
+
+        def last_plane(j0):
             gather(high[j0][:, 1, :], 3, j0, CHUNK)
-            nc.scalar.copy(x_woven[j0][:, :, 2:4], high[j0][:].rearrange("p t n -> p n t"))
+            for j, n in pieces:
+                if j0 <= j < j0 + CHUNK:
+                    nc.scalar.copy(x_woven[j][:, :, 2:4], high[j0][:, :, j - j0 : j - j0 + n].rearrange("p t n -> p n t"))
 
         wa_dealt = keep.tile([P, N], U32, name="wa_dealt", align_bytes=64)
-        nc.vector.tensor_copy(
-            wa_dealt[:].bitcast(I32).rearrange("p (t q) -> p t q", t=PACK), wa_raw[:].bitcast(I32).rearrange("p (q t) -> p t q", t=PACK)
-        )
-
-        x_codes, x_scales = {}, {}
-        for j0 in chunks:
-            codes = keep.tile([P, CHUNK], U32, name=f"x_codes{j0}", align_bytes=64)
-            scales = keep.tile([P, CHUNK], U8, name=f"x_scales{j0}", align_bytes=64)
-            nc.vector.quantize_mx(out=codes[:].bitcast(FP8X4), scales=scales[:], in_=x_woven[j0][:].rearrange("p n t -> p (n t)"))
-            x_codes[j0] = codes
-            x_scales[j0] = scales
 
         y_rows = out_0.rearrange("(p t) j -> p t j", t=PACK)
         y_words = out_1[0].rearrange("p j b -> p (j b)").bitcast(I32)
         y_scales = keep.tile([P, J], U8, name="y_scales", align_bytes=64)
-        y_woven = {}
-        for j0 in chunks:
-            y = keep.tile([P, PACK, CHUNK], F32, name=f"y{j0}")
-            for u in range(2):
-                bank = psum.tile([P, 2, CHUNK], F32, name="z_bank", tag="bank")
-                for s in range(2):
-                    t = 2 * u + s
-                    if j0 >= HALF:
-                        w_codes = wb_dealt[:, 2 * P * t : 2 * P * (t + 1)].bitcast(FP4X4)
-                        w_scales = sc_dealt[:, P * t : P * (t + 1)]
-                    else:
-                        w_codes = wa_dealt[:, P * t : P * (t + 1)].bitcast(FP8X4)
-                        w_scales = sc_dealt[WA_ROW:P, P * t : P * (t + 1)]
-                    nc.tensor.matmul_mx(
-                        out=bank[:, s, :],
-                        lhsT=w_codes,
-                        lhsT_scale=w_scales,
-                        rhs=x_codes[j0][:].bitcast(FP8X4),
-                        rhs_scale=x_scales[j0][:],
-                        start=True,
-                        stop=True,
-                    )
-                nc.vector.scalar_tensor_tensor(
-                    y[:, 2 * u : 2 * u + 2, :],
-                    bank[:],
-                    0.0,
-                    rw_all[:, j0 : j0 + CHUNK].unsqueeze(1).to_broadcast([P, 2, CHUNK]),
-                    ALU.max,
-                    ALU.mult,
-                )
-            nc.sync.dma_start(y_rows[:, :, j0 : j0 + CHUNK], y[:])
-            woven = keep.tile([P, CHUNK, PACK], BF16, name=f"y_woven{j0}", align_bytes=64)
-            nc.scalar.copy(woven[:].rearrange("p (c i) t -> p c t i", i=4), y[:].rearrange("p t (c i) -> p c t i", i=4))
-            y_woven[j0] = woven
+        x_mx, y_woven = {}, {}
 
-        for j0 in chunks:
-            codes = keep.tile([P, CHUNK], U32, name=f"y_codes{j0}", align_bytes=64)
-            nc.vector.quantize_mx(
-                out=codes[:].bitcast(FP8X4), scales=y_scales[:, j0 : j0 + CHUNK], in_=y_woven[j0][:].rearrange("p n t -> p (n t)")
+        def quantize_x(j, n):
+            codes = keep.tile([P, n], U32, name=f"x_codes{j}", align_bytes=64)
+            scales = keep.tile([P, n], U8, name=f"x_scales{j}", align_bytes=64)
+            nc.vector.quantize_mx(out=codes[:].bitcast(FP8X4), scales=scales[:], in_=x_woven[j].rearrange("p n t -> p (n t)"))
+            for c in range(0, n, P):
+                x_mx[j + c] = (codes[:, c : c + P], scales[:, c : c + P])
+
+        def result_tiles(j, n):
+            y = keep.tile([P, PACK, n], F32, name=f"y{j}")
+            woven = keep.tile([P, n, PACK], BF16, name=f"y_woven{j}", align_bytes=64)
+            y_woven[j] = (y, woven, n)
+
+        def multiply(j0, c):
+            y, woven, n = y_woven[j0]
+            j = j0 + c
+            codes, scales = x_mx[j]
+            bank = psum.tile([P, PACK, P], F32, name="z_bank", tag="bank")
+            for t in range(PACK):
+                if j >= HALF:
+                    w_codes = wb_dealt[:, 2 * P * t : 2 * P * (t + 1)].bitcast(FP4X4)
+                    w_scales = wb_plane[:, P * t : P * (t + 1)]
+                else:
+                    w_codes = wa_dealt[:, P * t : P * (t + 1)].bitcast(FP8X4)
+                    w_scales = wa_plane[:, P * t : P * (t + 1)]
+                nc.tensor.matmul_mx(
+                    out=bank[:, t, :],
+                    lhsT=w_codes,
+                    lhsT_scale=w_scales,
+                    rhs=codes.bitcast(FP8X4),
+                    rhs_scale=scales,
+                    start=True,
+                    stop=True,
+                )
+            nc.vector.scalar_tensor_tensor(
+                y[:, :, c : c + P],
+                bank[:],
+                0.0,
+                rw_slots(j).unsqueeze(1).to_broadcast([P, PACK, P]),
+                ALU.max,
+                ALU.mult,
             )
-            nc.sync.dma_start(y_words[:, j0 : j0 + CHUNK], codes[:].bitcast(I32))
+            if c + P == n:
+                nc.sync.dma_start(y_rows[:, :, j0 : j0 + n], y[:])
+            nc.scalar.copy(
+                woven[:, c : c + P, :].rearrange("p (c i) t -> p c t i", i=4),
+                y[:, :, c : c + P].rearrange("p t (c i) -> p c t i", i=4),
+            )
+
+        def quantize_y(j):
+            y, woven, n = y_woven[j]
+            codes = keep.tile([P, n], U32, name=f"y_codes{j}", align_bytes=64)
+            nc.vector.quantize_mx(
+                out=codes[:].bitcast(FP8X4), scales=y_scales[:, j : j + n], in_=woven[:].rearrange("p n t -> p (n t)")
+            )
+            nc.sync.dma_start(y_words[:, j : j + n], codes[:].bitcast(I32))
+
+        for j, n in [(c0, P), (c0 + P, P), (c1, CHUNK), (c2, CHUNK), (c3, P), (c3 + P, P)]:
+            result_tiles(j, n)
+        last_plane(c0)
+        last_plane(c1)
+        quantize_x(c0, P)
+        last_plane(c2)
+        quantize_x(c0 + P, P)
+        multiply(c0, 0)
+        quantize_x(c1, CHUNK)
+        multiply(c0 + P, 0)
+        last_plane(c3)
+        multiply(c1, 0)
+        quantize_x(c2, CHUNK)
+        nc.vector.tensor_copy(
+            wa_dealt[:].bitcast(I32).rearrange("p (t q) -> p t q", t=PACK), wa_raw[:].bitcast(I32).rearrange("p (q t) -> p t q", t=PACK)
+        )
+        multiply(c1, P)
+        quantize_x(c3, CHUNK)
+        multiply(c2, 0)
+        quantize_y(c0)
+        quantize_y(c0 + P)
+        multiply(c2, P)
+        multiply(c3, 0)
+        quantize_y(c1)
+        multiply(c3 + P, 0)
+        quantize_y(c2)
+        quantize_y(c3)
+        quantize_y(c3 + P)
         for q in range(4):
             queue = nc.scalar if q % 2 == 0 else nc.sync
             queue.dma_start(out_2[0, 4 * q : 4 * q + 4, :].bitcast(I32), y_scales[32 * q : 32 * q + 4, :].bitcast(I32))

@@ -41,7 +41,7 @@ def tile_list_halves_of_the_list_pl_kernel(tc, xf, wa_words, wa_scales, wb_words
 
         nc.sync.dma_start(sc_raw[0:16, :].bitcast(I32), wb_scales[0].bitcast(I32))
         nc.sync.dma_start(sc_raw[16:32, :].bitcast(I32), wa_scales[0].bitcast(I32))
-        wb_raw = keep.tile([P, 2 * N], U8, name="wb_raw", tag="w_raw", align_bytes=64)
+        wb_raw = keep.tile([P, 2 * N], U8, name="wb_raw", align_bytes=64)
         nc.sync.dma_start(wb_raw[:].bitcast(I32), wb_words[0].bitcast(I32))
         x_rows = xf.rearrange("(p t) n -> t p n", t=PACK)
         planes = [keep.tile([P, T], F32, name=f"plane{t}") for t in range(PACK)]
@@ -51,6 +51,8 @@ def tile_list_halves_of_the_list_pl_kernel(tc, xf, wa_words, wa_scales, wb_words
         nc.sync.dma_start(rw_cols[:], rw.rearrange("o (p m) -> (o p) m", p=P))
         for t in range(1, PACK):
             nc.sync.dma_start(planes[t][:], x_rows[t])
+        wa_raw = keep.tile([P, N], U32, name="wa_raw", align_bytes=64)
+        nc.sync.dma_start(wa_raw[:].bitcast(I32), wa_words[0].rearrange("p n b -> p (n b)").bitcast(I32))
 
         wb_plane = keep.tile([P, N], U8, name="wb_plane", align_bytes=64)
         nc.vector.tensor_copy(wb_plane[:].rearrange("p (t q) -> p t q", t=PACK), sc_raw[:].rearrange("p (q t) -> p t q", t=PACK))
@@ -62,76 +64,60 @@ def tile_list_halves_of_the_list_pl_kernel(tc, xf, wa_words, wa_scales, wb_words
         nc.vector.tensor_copy(
             wb_dealt[:].rearrange("p (t q b) -> p t q b", t=PACK, b=2), wb_raw[:].rearrange("p (q t b) -> p t q b", t=PACK, b=2)
         )
-        wa_raw = keep.tile([P, N], U32, name="wa_raw", tag="w_raw", align_bytes=64)
-        nc.sync.dma_start(wa_raw[:].bitcast(I32), wa_words[0].rearrange("p n b -> p (n b)").bitcast(I32))
-
-        high = {j0: keep.tile([P, 2, CHUNK], F32, name=f"high{j0}", align_bytes=64) for j0 in chunks}
-        low = {h: keep.tile([P, 2, HALF], F32, name=f"low{h}") for h in (HALF, 0)}
 
         ident = keep.tile([P, P], F32, name="ident")
         make_identity(nc, ident[:])
-        rw_rest = keep.tile([P, c0], F32, name="rw_rest")
-        rw_first = high[c3][:, 1, :]
-        split = c0 // 8
+        rw_all = keep.tile([P, J], F32, name="rw_all")
         for h in range(2):
             bank = psum.tile([P, 4, P], F32, name="rw_bank", tag="bank")
             for m in range(4):
                 nc.tensor.transpose(bank[:, m, :], rw_cols[:, 4 * h + m : 4 * h + m + 1].to_broadcast([P, P]), ident[:])
-            by_slot = bank[:].rearrange("q m p -> q p m")
-            nc.scalar.copy(rw_first.rearrange("q (p m) -> q p m", m=8)[:, :, 4 * h : 4 * h + 4], by_slot[:, split:P, :])
-            nc.scalar.copy(rw_rest[:].rearrange("q (p m) -> q p m", m=8)[:, :, 4 * h : 4 * h + 4], by_slot[:, 0:split, :])
-
-        def rw_slots(j):
-            return rw_first[:, j - c0 : j - c0 + P] if j >= c0 else rw_rest[:, j : j + P]
+            nc.scalar.copy(rw_all[:].rearrange("q (p m) -> q p m", m=8)[:, :, 4 * h : 4 * h + 4], bank[:].rearrange("q m p -> q p m"))
 
         def gather(out, t, j0, n):
             nc.vector.tensor_copy(out, planes[t][:].indirect(offsets[:, j0 // PER_COL : (j0 + n) // PER_COL]))
 
-        pieces = [(c0, P), (c0 + P, P), (c1, CHUNK), (c2, CHUNK), (c3, CHUNK)]
-        x_woven = {j: keep.tile([P, n, PACK], BF16, name=f"x_woven{j}", align_bytes=64)[:] for j, n in pieces[1:]}
-        x_woven[c0] = high[c2][:, 1, :].bitcast(BF16).rearrange("p (n t) -> p n t", t=PACK)
+        low = keep.tile([P, 2, J], F32, name="low")
+        high = {j0: keep.tile([P, 2, CHUNK], F32, name=f"high{j0}")[:] for j0 in chunks[:-1]}
+        x_woven = {j0: keep.tile([P, CHUNK, PACK], BF16, name=f"x_woven{j0}", tag=f"x_woven{j0}", align_bytes=64)[:] for j0 in chunks[1:]}
+        shared = keep.tile([P, 3, CHUNK], F32, name="shared", align_bytes=64)
+        high[c3] = shared[:, 0:2, :]
+        x_woven[c0] = shared[:, 1:3, :].rearrange("p r n -> p (r n)").bitcast(BF16).rearrange("p (n t) -> p n t", t=PACK)
 
-        for h in low:
-            gather(low[h][:, 0, :], 0, h, HALF)
-        for h in low:
-            gather(low[h][:, 1, :], 1, h, HALF)
-            for j, n in pieces:
-                if h <= j < h + HALF:
-                    nc.scalar.copy(x_woven[j][:, :, 0:2], low[h][:, :, j - h : j - h + n].rearrange("p t n -> p n t"))
+        gather(low[:, 0, :], 0, 0, J)
+        for h in (HALF, 0):
+            gather(low[:, 1, h : h + HALF], 1, h, HALF)
+        for j0 in chunks:
+            nc.scalar.copy(x_woven[j0][:, :, 0:2], low[:, :, j0 : j0 + CHUNK].rearrange("p t n -> p n t"))
         for j0 in chunks:
             gather(high[j0][:, 0, :], 2, j0, CHUNK)
 
         def last_plane(j0):
             gather(high[j0][:, 1, :], 3, j0, CHUNK)
-            for j, n in pieces:
-                if j0 <= j < j0 + CHUNK:
-                    nc.scalar.copy(x_woven[j][:, :, 2:4], high[j0][:, :, j - j0 : j - j0 + n].rearrange("p t n -> p n t"))
-
-        wa_dealt = keep.tile([P, N], U32, name="wa_dealt", align_bytes=64)
+            nc.scalar.copy(x_woven[j0][:, :, 2:4], high[j0].rearrange("p t n -> p n t"))
 
         y_rows = out_0.rearrange("(p t) j -> p t j", t=PACK)
         y_words = out_1[0].rearrange("p j b -> p (j b)").bitcast(I32)
         y_scales = keep.tile([P, J], U8, name="y_scales", align_bytes=64)
         x_mx, y_woven = {}, {}
 
-        def quantize_x(j, n):
-            codes = keep.tile([P, n], U32, name=f"x_codes{j}", align_bytes=64)
-            scales = keep.tile([P, n], U8, name=f"x_scales{j}", align_bytes=64)
-            nc.vector.quantize_mx(out=codes[:].bitcast(FP8X4), scales=scales[:], in_=x_woven[j].rearrange("p n t -> p (n t)"))
-            for c in range(0, n, P):
-                x_mx[j + c] = (codes[:, c : c + P], scales[:, c : c + P])
+        def quantize_x(j0):
+            codes = keep.tile([P, CHUNK], U32, name=f"x_codes{j0}", align_bytes=64)
+            scales = keep.tile([P, CHUNK], U8, name=f"x_scales{j0}", align_bytes=64)
+            nc.vector.quantize_mx(out=codes[:].bitcast(FP8X4), scales=scales[:], in_=x_woven[j0].rearrange("p n t -> p (n t)"))
+            x_mx[j0] = (codes, scales)
 
-        def result_tiles(j, n):
-            y = keep.tile([P, PACK, n], F32, name=f"y{j}")
-            woven = keep.tile([P, n, PACK], BF16, name=f"y_woven{j}", align_bytes=64)
-            y_woven[j] = (y, woven, n)
+        y_tiles = {}
 
-        def multiply(j0, c):
-            y, woven, n = y_woven[j0]
+        def multiply(j0, c, n, t0, nt):
             j = j0 + c
-            codes, scales = x_mx[j]
-            bank = psum.tile([P, PACK, P], F32, name="z_bank", tag="bank")
-            for t in range(PACK):
+            if t0 == 0:
+                y_tiles[j] = keep.tile([P, PACK, n], F32, name=f"y{j}")
+            y = y_tiles[j]
+            codes, scales = x_mx[j0]
+            bank = psum.tile([P, nt, n], F32, name="z_bank", tag="bank")
+            for s in range(nt):
+                t = t0 + s
                 if j >= HALF:
                     w_codes = wb_dealt[:, 2 * P * t : 2 * P * (t + 1)].bitcast(FP4X4)
                     w_scales = wb_plane[:, P * t : P * (t + 1)]
@@ -139,65 +125,69 @@ def tile_list_halves_of_the_list_pl_kernel(tc, xf, wa_words, wa_scales, wb_words
                     w_codes = wa_dealt[:, P * t : P * (t + 1)].bitcast(FP8X4)
                     w_scales = wa_plane[:, P * t : P * (t + 1)]
                 nc.tensor.matmul_mx(
-                    out=bank[:, t, :],
+                    out=bank[:, s, :],
                     lhsT=w_codes,
                     lhsT_scale=w_scales,
-                    rhs=codes.bitcast(FP8X4),
-                    rhs_scale=scales,
+                    rhs=codes[:, c : c + n].bitcast(FP8X4),
+                    rhs_scale=scales[:, c : c + n],
                     start=True,
                     stop=True,
                 )
             nc.vector.scalar_tensor_tensor(
-                y[:, :, c : c + P],
+                y[:, t0 : t0 + nt, :],
                 bank[:],
                 0.0,
-                rw_slots(j).unsqueeze(1).to_broadcast([P, PACK, P]),
+                rw_all[:, j : j + n].unsqueeze(1).to_broadcast([P, nt, n]),
                 ALU.max,
                 ALU.mult,
             )
-            if c + P == n:
-                nc.sync.dma_start(y_rows[:, :, j0 : j0 + n], y[:])
-            nc.scalar.copy(
-                woven[:, c : c + P, :].rearrange("p (c i) t -> p c t i", i=4),
-                y[:, :, c : c + P].rearrange("p t (c i) -> p c t i", i=4),
+            nc.sync.dma_start(y_rows[:, t0 : t0 + nt, j : j + n], y[:, t0 : t0 + nt, :])
+
+        def weave_y(j0, c, n, copy):
+            if c == 0:
+                y_woven[j0] = keep.tile([P, CHUNK, PACK], BF16, name=f"y_woven{j0}", align_bytes=64)
+            copy(
+                y_woven[j0][:, c : c + n, :].rearrange("p (g i) t -> p g t i", i=4),
+                y_tiles[j0 + c][:].rearrange("p t (g i) -> p g t i", i=4),
             )
 
         def quantize_y(j):
-            y, woven, n = y_woven[j]
+            woven, n = y_woven[j], CHUNK
             codes = keep.tile([P, n], U32, name=f"y_codes{j}", align_bytes=64)
             nc.vector.quantize_mx(
                 out=codes[:].bitcast(FP8X4), scales=y_scales[:, j : j + n], in_=woven[:].rearrange("p n t -> p (n t)")
             )
             nc.sync.dma_start(y_words[:, j : j + n], codes[:].bitcast(I32))
 
-        for j, n in [(c0, P), (c0 + P, P), (c1, CHUNK), (c2, CHUNK), (c3, P), (c3 + P, P)]:
-            result_tiles(j, n)
         last_plane(c0)
         last_plane(c1)
-        quantize_x(c0, P)
         last_plane(c2)
-        quantize_x(c0 + P, P)
-        multiply(c0, 0)
-        quantize_x(c1, CHUNK)
-        multiply(c0 + P, 0)
+        quantize_x(c0)
         last_plane(c3)
-        multiply(c1, 0)
-        quantize_x(c2, CHUNK)
+        quantize_x(c1)
+        multiply(c0, 0, CHUNK, 0, 2)
+        multiply(c0, 0, CHUNK, 2, 2)
+        weave_y(c0, 0, CHUNK, nc.scalar.copy)
+        quantize_x(c2)
+        multiply(c1, 0, CHUNK, 0, 2)
+        wa_dealt = keep.tile([P, N], U32, name="wa_dealt", tag=f"x_woven{c2}", align_bytes=64)
         nc.vector.tensor_copy(
             wa_dealt[:].bitcast(I32).rearrange("p (t q) -> p t q", t=PACK), wa_raw[:].bitcast(I32).rearrange("p (q t) -> p t q", t=PACK)
         )
-        multiply(c1, P)
-        quantize_x(c3, CHUNK)
-        multiply(c2, 0)
+        multiply(c1, 0, CHUNK, 2, 2)
+        weave_y(c1, 0, CHUNK, nc.scalar.copy)
+        quantize_x(c3)
+        multiply(c2, 0, CHUNK, 0, 2)
+        multiply(c2, 0, CHUNK, 2, 2)
+        weave_y(c2, 0, CHUNK, nc.scalar.copy)
+        multiply(c3, 0, P, 0, PACK)
+        weave_y(c3, 0, P, nc.scalar.copy)
+        multiply(c3, P, P, 0, PACK)
         quantize_y(c0)
-        quantize_y(c0 + P)
-        multiply(c2, P)
-        multiply(c3, 0)
+        weave_y(c3, P, P, nc.vector.tensor_copy)
         quantize_y(c1)
-        multiply(c3 + P, 0)
         quantize_y(c2)
         quantize_y(c3)
-        quantize_y(c3 + P)
         for q in range(4):
             queue = nc.scalar if q % 2 == 0 else nc.sync
             queue.dma_start(out_2[0, 4 * q : 4 * q + 4, :].bitcast(I32), y_scales[32 * q : 32 * q + 4, :].bitcast(I32))

@@ -77,24 +77,29 @@ def tile_list_halves_of_the_list_pl_kernel(tc, xf, wa_words, wa_scales, wb_words
         def gather(out, t, j0, n):
             nc.vector.tensor_copy(out, planes[t][:].indirect(offsets[:, j0 // PER_COL : (j0 + n) // PER_COL]))
 
-        low = keep.tile([P, 2, J], F32, name="low")
+        low = {h: keep.tile([P, 2, HALF], F32, name=f"low{h}") for h in (HALF, 0)}
         high = {j0: keep.tile([P, 2, CHUNK], F32, name=f"high{j0}")[:] for j0 in chunks[:-1]}
         x_woven = {j0: keep.tile([P, CHUNK, PACK], BF16, name=f"x_woven{j0}", tag=f"x_woven{j0}", align_bytes=64)[:] for j0 in chunks[1:]}
         shared = keep.tile([P, 3, CHUNK], F32, name="shared", align_bytes=64)
         high[c3] = shared[:, 0:2, :]
         x_woven[c0] = shared[:, 1:3, :].rearrange("p r n -> p (r n)").bitcast(BF16).rearrange("p (n t) -> p n t", t=PACK)
 
-        gather(low[:, 0, :], 0, 0, J)
-        for h in (HALF, 0):
-            gather(low[:, 1, h : h + HALF], 1, h, HALF)
+        def weave_pair(j0, t0, pair):
+            nc.scalar.copy(
+                x_woven[j0][:, :, t0 : t0 + 2].rearrange("p (g i) t -> p g t i", i=2), pair.rearrange("p t (g i) -> p g t i", i=2)
+            )
+
+        for t in range(2):
+            for h in low:
+                gather(low[h][:, t, :], t, h, HALF)
         for j0 in chunks:
-            nc.scalar.copy(x_woven[j0][:, :, 0:2], low[:, :, j0 : j0 + CHUNK].rearrange("p t n -> p n t"))
+            weave_pair(j0, 0, low[j0 - j0 % HALF][:, :, j0 % HALF : j0 % HALF + CHUNK])
         for j0 in chunks:
             gather(high[j0][:, 0, :], 2, j0, CHUNK)
 
         def last_plane(j0):
             gather(high[j0][:, 1, :], 3, j0, CHUNK)
-            nc.scalar.copy(x_woven[j0][:, :, 2:4], high[j0].rearrange("p t n -> p n t"))
+            weave_pair(j0, 2, high[j0])
 
         y_rows = out_0.rearrange("(p t) j -> p t j", t=PACK)
         y_words = out_1[0].rearrange("p j b -> p (j b)").bitcast(I32)
@@ -147,17 +152,21 @@ def tile_list_halves_of_the_list_pl_kernel(tc, xf, wa_words, wa_scales, wb_words
             if c == 0:
                 y_woven[j0] = keep.tile([P, CHUNK, PACK], BF16, name=f"y_woven{j0}", align_bytes=64)
             copy(
-                y_woven[j0][:, c : c + n, :].rearrange("p (g i) t -> p g t i", i=4),
-                y_tiles[j0 + c][:].rearrange("p t (g i) -> p g t i", i=4),
+                y_woven[j0][:, c : c + n, :].rearrange("p (g i) t -> p g t i", i=2),
+                y_tiles[j0][:, :, c : c + n].rearrange("p t (g i) -> p g t i", i=2),
             )
 
+        y_codes = {h: keep.tile([P, HALF], U32, name=f"y_codes{h}", align_bytes=64) for h in (HALF, 0)}
+
         def quantize_y(j):
-            woven, n = y_woven[j], CHUNK
-            codes = keep.tile([P, n], U32, name=f"y_codes{j}", align_bytes=64)
+            h = j - j % HALF
             nc.vector.quantize_mx(
-                out=codes[:].bitcast(FP8X4), scales=y_scales[:, j : j + n], in_=woven[:].rearrange("p n t -> p (n t)")
+                out=y_codes[h][:, j - h : j - h + CHUNK].bitcast(FP8X4),
+                scales=y_scales[:, j : j + CHUNK],
+                in_=y_woven[j][:].rearrange("p n t -> p (n t)"),
             )
-            nc.sync.dma_start(y_words[:, j : j + n], codes[:].bitcast(I32))
+            if j == h:
+                nc.sync.dma_start(y_words[:, h : h + HALF], y_codes[h][:].bitcast(I32))
 
         last_plane(c0)
         last_plane(c1)
@@ -172,7 +181,8 @@ def tile_list_halves_of_the_list_pl_kernel(tc, xf, wa_words, wa_scales, wb_words
         multiply(c1, 0, CHUNK, 0, 2)
         wa_dealt = keep.tile([P, N], U32, name="wa_dealt", tag=f"x_woven{c2}", align_bytes=64)
         nc.vector.tensor_copy(
-            wa_dealt[:].bitcast(I32).rearrange("p (t q) -> p t q", t=PACK), wa_raw[:].bitcast(I32).rearrange("p (q t) -> p t q", t=PACK)
+            wa_dealt[:].bitcast(I32).rearrange("p (t g i) -> p g t i", t=PACK, i=2),
+            wa_raw[:].bitcast(I32).rearrange("p (g i t) -> p g t i", t=PACK, i=2),
         )
         multiply(c1, 0, CHUNK, 2, 2)
         weave_y(c1, 0, CHUNK, nc.scalar.copy)
@@ -180,9 +190,9 @@ def tile_list_halves_of_the_list_pl_kernel(tc, xf, wa_words, wa_scales, wb_words
         multiply(c2, 0, CHUNK, 0, 2)
         multiply(c2, 0, CHUNK, 2, 2)
         weave_y(c2, 0, CHUNK, nc.scalar.copy)
-        multiply(c3, 0, P, 0, PACK)
+        multiply(c3, 0, CHUNK, 0, 2)
+        multiply(c3, 0, CHUNK, 2, 2)
         weave_y(c3, 0, P, nc.scalar.copy)
-        multiply(c3, P, P, 0, PACK)
         quantize_y(c0)
         weave_y(c3, P, P, nc.vector.tensor_copy)
         quantize_y(c1)

from contextlib import ExitStack

import concourse.mybir as mybir
from concourse.masks import make_identity

K, T, J, N = 512, 2048, 1024, 512
FLOPS = 2 * K * N * J

F32 = mybir.dt.float32
BF16 = mybir.dt.bfloat16
I32 = mybir.dt.int32
U32 = mybir.dt.uint32
U16 = mybir.dt.uint16
U8 = mybir.dt.uint8
FP8X4 = mybir.dt.float8_e4m3fn_x4
FP4X4 = mybir.dt.float4_e2m1fn_x4
ALU = mybir.AluOpType

P = 128
PACK = 4
HALF = J // 2
CHUNK = 256
PER_COL = 16


def tile_list_halves_of_the_list_pl_kernel(tc, xf, wa_words, wa_scales, wb_words, wb_scales, rw, offs, out_0, out_1, out_2):
    nc = tc.nc
    chunks = list(range(J - CHUNK, -1, -CHUNK))
    c0, c1, c2, c3 = chunks

    with ExitStack() as ctx:
        keep = ctx.enter_context(tc.tile_pool(name="keep", bufs=1))
        psum = ctx.enter_context(tc.psum_pool(name="psum", bufs=8))

        offsets = keep.tile([P, J // PER_COL], U16, name="offsets")
        sc_raw = keep.tile([P, N], U8, name="sc_raw", align_bytes=64)
        nc.gpsimd.memset(sc_raw[32:64, :].bitcast(I32), 0)
        nc.gpsimd.memset(sc_raw[64:P, :].bitcast(I32), 0)
        wa_plane = keep.tile([P, N], U8, name="wa_plane", align_bytes=64)
        nc.gpsimd.memset(wa_plane[:].bitcast(I32), 0)

        nc.sync.dma_start(sc_raw[0:16, :].bitcast(I32), wb_scales[0].bitcast(I32))
        nc.sync.dma_start(sc_raw[16:32, :].bitcast(I32), wa_scales[0].bitcast(I32))
        wb_raw = keep.tile([P, 2 * N], U8, name="wb_raw", align_bytes=64)
        nc.sync.dma_start(wb_raw[:].bitcast(I32), wb_words[0].bitcast(I32))
        x_rows = xf.rearrange("(p t) n -> t p n", t=PACK)
        planes = [keep.tile([P, T], F32, name=f"plane{t}") for t in range(PACK)]
        nc.sync.dma_start(planes[0][:], x_rows[0])
        nc.sync.dma_start(offsets[:], offs)
        rw_cols = keep.tile([P, J // P], F32, name="rw_cols")
        nc.sync.dma_start(rw_cols[:], rw.rearrange("o (p m) -> (o p) m", p=P))
        for t in range(1, PACK):
            nc.sync.dma_start(planes[t][:], x_rows[t])
        wa_raw = keep.tile([P, N], U32, name="wa_raw", align_bytes=64)
        nc.sync.dma_start(wa_raw[:].bitcast(I32), wa_words[0].rearrange("p n b -> p (n b)").bitcast(I32))

        wb_plane = keep.tile([P, N], U8, name="wb_plane", align_bytes=64)
        nc.vector.tensor_copy(wb_plane[:].rearrange("p (t q) -> p t q", t=PACK), sc_raw[:].rearrange("p (q t) -> p t q", t=PACK))
        for q in range(1, 4):
            nc.sync.dma_start(wb_plane[32 * q : 32 * q + 4, :].bitcast(I32), wb_plane[4 * q : 4 * q + 4, :].bitcast(I32))
        for q in range(4):
            nc.sync.dma_start(wa_plane[32 * q : 32 * q + 4, :].bitcast(I32), wb_plane[16 + 4 * q : 20 + 4 * q, :].bitcast(I32))
        wb_dealt = keep.tile([P, 2 * N], U8, name="wb_dealt", align_bytes=64)
        nc.vector.tensor_copy(
            wb_dealt[:].rearrange("p (t q b) -> p t q b", t=PACK, b=2), wb_raw[:].rearrange("p (q t b) -> p t q b", t=PACK, b=2)
        )

        ident = keep.tile([P, P], F32, name="ident")
        make_identity(nc, ident[:])
        rw_all = keep.tile([P, J], F32, name="rw_all")
        for h in range(2):
            bank = psum.tile([P, 4, P], F32, name="rw_bank", tag="bank")
            for m in range(4):
                nc.tensor.transpose(bank[:, m, :], rw_cols[:, 4 * h + m : 4 * h + m + 1].to_broadcast([P, P]), ident[:])
            nc.scalar.copy(rw_all[:].rearrange("q (p m) -> q p m", m=8)[:, :, 4 * h : 4 * h + 4], bank[:].rearrange("q m p -> q p m"))

        def gather(out, t, j0, n):
            nc.vector.tensor_copy(out, planes[t][:].indirect(offsets[:, j0 // PER_COL : (j0 + n) // PER_COL]))

        low = {h: keep.tile([P, 2, HALF], F32, name=f"low{h}") for h in (HALF, 0)}
        high = {j0: keep.tile([P, 2, CHUNK], F32, name=f"high{j0}")[:] for j0 in chunks[:-1]}
        x_woven = {j0: keep.tile([P, CHUNK, PACK], BF16, name=f"x_woven{j0}", tag=f"x_woven{j0}", align_bytes=64)[:] for j0 in chunks[1:]}
        shared = keep.tile([P, 3, CHUNK], F32, name="shared", align_bytes=64)
        high[c3] = shared[:, 0:2, :]
        x_woven[c0] = shared[:, 1:3, :].rearrange("p r n -> p (r n)").bitcast(BF16).rearrange("p (n t) -> p n t", t=PACK)

        def weave_pair(j0, t0, pair):
            nc.scalar.copy(
                x_woven[j0][:, :, t0 : t0 + 2].rearrange("p (g i) t -> p g t i", i=2), pair.rearrange("p t (g i) -> p g t i", i=2)
            )

        for t in range(2):
            for h in low:
                gather(low[h][:, t, :], t, h, HALF)
        for j0 in chunks:
            weave_pair(j0, 0, low[j0 - j0 % HALF][:, :, j0 % HALF : j0 % HALF + CHUNK])
        for j0 in chunks:
            gather(high[j0][:, 0, :], 2, j0, CHUNK)

        def last_plane(j0):
            gather(high[j0][:, 1, :], 3, j0, CHUNK)
            weave_pair(j0, 2, high[j0])

        y_rows = out_0.rearrange("(p t) j -> p t j", t=PACK)
        y_words = out_1[0].rearrange("p j b -> p (j b)").bitcast(I32)
        y_scales = keep.tile([P, J], U8, name="y_scales", align_bytes=64)
        x_mx, y_woven = {}, {}

        def quantize_x(j0):
            codes = keep.tile([P, CHUNK], U32, name=f"x_codes{j0}", align_bytes=64)
            scales = keep.tile([P, CHUNK], U8, name=f"x_scales{j0}", align_bytes=64)
            nc.vector.quantize_mx(out=codes[:].bitcast(FP8X4), scales=scales[:], in_=x_woven[j0].rearrange("p n t -> p (n t)"))
            x_mx[j0] = (codes, scales)

        y_tiles = {}

        def multiply(j0, c, n, t0, nt):
            j = j0 + c
            if t0 == 0:
                y_tiles[j] = keep.tile([P, PACK, n], F32, name=f"y{j}")
            y = y_tiles[j]
            codes, scales = x_mx[j0]
            bank = psum.tile([P, nt, n], F32, name="z_bank", tag="bank")
            for s in range(nt):
                t = t0 + s
                if j >= HALF:
                    w_codes = wb_dealt[:, 2 * P * t : 2 * P * (t + 1)].bitcast(FP4X4)
                    w_scales = wb_plane[:, P * t : P * (t + 1)]
                else:
                    w_codes = wa_dealt[:, P * t : P * (t + 1)].bitcast(FP8X4)
                    w_scales = wa_plane[:, P * t : P * (t + 1)]
                nc.tensor.matmul_mx(
                    out=bank[:, s, :],
                    lhsT=w_codes,
                    lhsT_scale=w_scales,
                    rhs=codes[:, c : c + n].bitcast(FP8X4),
                    rhs_scale=scales[:, c : c + n],
                    start=True,
                    stop=True,
                )
            nc.vector.scalar_tensor_tensor(
                y[:, t0 : t0 + nt, :],
                bank[:],
                0.0,
                rw_all[:, j : j + n].unsqueeze(1).to_broadcast([P, nt, n]),
                ALU.max,
                ALU.mult,
            )
            nc.sync.dma_start(y_rows[:, t0 : t0 + nt, j : j + n], y[:, t0 : t0 + nt, :])

        def weave_y(j0, c, n, copy):
            if c == 0:
                y_woven[j0] = keep.tile([P, CHUNK, PACK], BF16, name=f"y_woven{j0}", align_bytes=64)
            copy(
                y_woven[j0][:, c : c + n, :].rearrange("p (g i) t -> p g t i", i=2),
                y_tiles[j0][:, :, c : c + n].rearrange("p t (g i) -> p g t i", i=2),
            )

        y_codes = {h: keep.tile([P, HALF], U32, name=f"y_codes{h}", align_bytes=64) for h in (HALF, 0)}

        def quantize_y(j):
            h = j - j % HALF
            nc.vector.quantize_mx(
                out=y_codes[h][:, j - h : j - h + CHUNK].bitcast(FP8X4),
                scales=y_scales[:, j : j + CHUNK],
                in_=y_woven[j][:].rearrange("p n t -> p (n t)"),
            )
            if j == h:
                nc.sync.dma_start(y_words[:, h : h + HALF], y_codes[h][:].bitcast(I32))

        last_plane(c0)
        last_plane(c1)
        last_plane(c2)
        quantize_x(c0)
        last_plane(c3)
        quantize_x(c1)
        multiply(c0, 0, CHUNK, 0, 2)
        multiply(c0, 0, CHUNK, 2, 2)
        weave_y(c0, 0, CHUNK, nc.scalar.copy)
        quantize_x(c2)
        multiply(c1, 0, CHUNK, 0, 2)
        wa_dealt = keep.tile([P, N], U32, name="wa_dealt", tag=f"x_woven{c2}", align_bytes=64)
        nc.vector.tensor_copy(
            wa_dealt[:].bitcast(I32).rearrange("p (t g i) -> p g t i", t=PACK, i=2),
            wa_raw[:].bitcast(I32).rearrange("p (g i t) -> p g t i", t=PACK, i=2),
        )
        multiply(c1, 0, CHUNK, 2, 2)
        weave_y(c1, 0, CHUNK, nc.scalar.copy)
        quantize_x(c3)
        multiply(c2, 0, CHUNK, 0, 2)
        multiply(c2, 0, CHUNK, 2, 2)
        weave_y(c2, 0, CHUNK, nc.scalar.copy)
        multiply(c3, 0, CHUNK, 0, 2)
        multiply(c3, 0, CHUNK, 2, 2)
        weave_y(c3, 0, P, nc.scalar.copy)
        quantize_y(c0)
        weave_y(c3, P, P, nc.vector.tensor_copy)
        quantize_y(c1)
        quantize_y(c2)
        quantize_y(c3)
        for q in range(4):
            queue = nc.scalar if q % 2 == 0 else nc.sync
            queue.dma_start(out_2[0, 4 * q : 4 * q + 4, :].bitcast(I32), y_scales[32 * q : 32 * q + 4, :].bitcast(I32))
